import numpy as np
CORES = [24,25,26,27,28,29,30,31,224,225,226,227,228,229,230,231]
N = 16
T, SQ = 2048, 1024
def entries(a): return a.T.reshape(-1)
def pack(v, P): return np.ascontiguousarray(np.asarray(v, np.int32).reshape(-1, P).T)
def lists(rng, how):
    d = np.concatenate([[0], rng.integers(1 - SQ // 2, SQ // 2, N - 1), [int(rng.integers(1 - SQ // 2, 1))]])
    if how == "lag": d[1:] = -SQ
    if how == "lead": d[1:N] = SQ; d[N] = 0
    if how == "runs": m = int(rng.integers(1, N - 2)); d[m] = -abs(d[m]); d[m + 1] = d[m] + SQ; d[m + 2] = d[m]
    if how == "skew": t = int(rng.integers(2, N - 1)); d[1:] = rng.integers(SQ // 2 + 1, SQ - 1, N); d[t + 1:] *= -1; d[t] = d[t - 1] + d[t + 1]
    n = SQ + np.diff(d)
    F = np.zeros((N, T), np.int64)
    for r in range(N):
        o = rng.permutation(T)
        if how == "runs": o = (T // 16 * rng.permutation(16)[:, None] + np.arange(T // 16)).reshape(-1)
        if how == "skew": o = np.concatenate([[0, T - 1], 1 + rng.permutation(T - 2)])
        F[r, o[:n[r]]] = 1
    return {"fl": np.stack([pack(f, 16) for f in F])}
def setup_inputs(rng):
    return dict({"x": rng.standard_normal((N, 128, T), dtype=np.float32), "st": rng.standard_normal((N, 128, SQ), dtype=np.float32)}, **lists(rng, "uniform"))
def setup_inputs_lag(rng):
    d = setup_inputs(rng); d.update(lists(rng, "lag"))
    for k in ("x", "st"): d[k] = (d[k].astype(np.float32) * 1048576.0).astype(d[k].dtype)
    return d
def setup_inputs_lead(rng):
    d = setup_inputs(rng); d.update(lists(rng, "lead"))
    for k in ("x", "st"): d[k] = (d[k].astype(np.float32) * (1 / 1024.0)).astype(d[k].dtype)
    return d
def setup_inputs_runs(rng):
    d = setup_inputs(rng); d.update(lists(rng, "runs"))
    return d
def setup_inputs_skew(rng):
    d = setup_inputs(rng); d.update(lists(rng, "skew"))
    return d
def check_inputs(x):
    bad = []
    if x["fl"].min() < 0 or x["fl"].max() >= 2: bad.append("fl out of range")
    if int(x["fl"].sum()) > N * SQ: bad.append("more flags than the stream has columns")
    c = np.concatenate([[0], np.cumsum([int(a.sum()) for a in x["fl"]])])
    if any(c[r] < (r - 1) * SQ or c[r + 1] > (r + 2) * SQ for r in range(N)): bad.append("a rank's share of the stream reaches beyond its neighbours' parts")
    return bad
def reference(x, st, fl):
    S = np.concatenate(list(st), axis=1); X = np.concatenate(list(x), axis=1)
    F = np.concatenate([entries(f) for f in fl]) > 0; c = np.cumsum(F) - F
    Y = np.where(F[None, :], S[:, np.minimum(c, N * SQ - 1)], X)
    return {"y": np.stack([Y[:, T * r:T * r + T] for r in range(N)])}

from concourse.bass import DstId, RemoteDMATransfer
from concourse.mybir import AluOpType, ActivationFunctionType

N, TC, SQ = 16, 2048, 1024
CW = 8
PIECES = (256, 768)
SOON = 3

SCRATCH = {
    "win": ("sbuf", [128, 3 * SQ + TC], "float32"),
    "yb": ("sbuf", [128, TC], "float32"),
    "rb": ("sbuf", [128, SQ], "float32"),
    "flc": ("sbuf", [128, 16], "int32"),
    "flp": ("sbuf", [128, 128], "int32"),
    "cnt": ("sbuf", [128, N * CW], "bfloat16"),
    "flb": ("sbuf", [128, 136], "bfloat16"),
    "kv": ("sbuf", [128, 128], "float32"),
    "kj": ("sbuf", [128, 128], "float32"),
    "kr": ("sbuf", [128, 128], "float32"),
    "kl": ("sbuf", [128, 128], "bfloat16"),
    "ku": ("sbuf", [128, 128], "bfloat16"),
    "one": ("sbuf", [128, 128], "bfloat16"),
    "zero": ("sbuf", [128, 256], "float32"),
    "nf": ("sbuf", [128, 128], "float32"),
    "uf": ("sbuf", [128, 128], "float32"),
    "sc": ("sbuf", [128, 256], "float32"),
    "mx": ("sbuf", [128, 128], "float32"),
    "off": ("sbuf", [128, 128], "uint16"),
    "pd": ("psum", [128, 512], "float32"),
    "pm": ("psum", [128, 512], "float32"),
}
SEMAPHORES = ["lf", "lg", "ls", "lx", "gi", "vk", "vc", "vf", "vn", "vu", "pe", "pem", "vs", "vm", "vo",
              "cin", "cf", "nb", "rl", "loc", "gv0", "gv1", "ga0", "ga1", "ys"]
PLANS = {}


def engines(mask):
    return [e for e in range(mask.bit_length()) if (mask >> e) & 1]


def as_mask(engs):
    return sum(1 << e for e in engs)


def plan(cores, topo):
    if "steps" in PLANS:
        return PLANS

    def one_chip(a, b):
        return topo.host(a) == topo.host(b) and topo.chip(a) == topo.chip(b)

    first = [c for c in cores if one_chip(c, cores[0])]
    second = [c for c in cores if c not in first]
    a, b = first[-1], second[0]
    fwd = [c for c in first if topo.may_write(c, b) and topo.die(c) != topo.die(a)]
    best = {}
    for c in second:
        if c != b and topo.may_write(c, a):
            best[topo.die(c)] = c
    rel = sorted(best.values())
    rw = SQ // len(rel)
    steps = {}
    for r, c in enumerate(cores):
        mine = first if c in first else second
        others = [d for d in mine if d != c and (d in fwd or cores.index(d) > r)]
        others.sort(key=lambda d: (d not in fwd, cores.index(d)))
        sides = [(cores[d], col) for d, col in ((r - 1, 2 * SQ), (r + 1, 0)) if 0 <= d < N]
        sides = [s for s in sides if topo.may_write(c, s[0])]

        def count(ds):
            return [("cnt", [(ds, "cnt", CW * r, "cnt", CW * r, CW, topo.mask(c, ds[0]), "cin")])] if ds else []

        def one(d, col):
            return ("st", [([d], "win", SQ, "win", col, SQ, topo.mask(c, d), "nb")])

        def both():
            call, used = [], 0
            for d, col in sides:
                if not one_chip(c, d):
                    used |= topo.mask(c, d)
                    call.append(([d], "win", SQ, "win", col, SQ, topo.mask(c, d), "nb"))
            near = [s for s in sides if one_chip(c, s[0])]
            for i, (d, col) in enumerate(near):
                free = [e for e in engines(topo.mask(c, d)) if not (used >> e) & 1]
                call.append(([d], "win", SQ, "win", col, SQ, as_mask(free[i::len(near)]), "nb"))
            return [("st", call)]

        if c in fwd:
            dd = second[fwd.index(c)::len(fwd)]
            out = count(others) + [one(*sides[0])]
            out += [("cin", [(dd, "cnt", 0, "cnt", 0, CW * len(first), topo.mask(c, dd[0]), "cf")])]
            out += [one(*s) for s in sides[1:]]
        elif c in first:
            out = count(others) + both()
        else:
            out = count(others[:SOON])
            if c == b:
                engs = engines(topo.mask(c, rel[0]))
                out += [("st", [([x], "win", SQ + i * rw, "rb", 0, rw, as_mask(engs[i::len(rel)]), "rl")
                                for i, x in enumerate(rel)])]
            out += both() + count(others[SOON:])
            if c in rel:
                out += [("rl", [([a], "rb", 0, "win", 2 * SQ + rel.index(c) * rw, rw, topo.mask(c, a), "nb")])]
        steps[c] = out
    PLANS["steps"] = steps
    return PLANS


def rank_program(g, core, T, topo):
    r = T.rank_of(core)
    if r is None:
        return
    S, A, F = T.sem, AluOpType, ActivationFunctionType
    steps = plan(list(T.cores), topo)["steps"]

    def total(sem):
        return sum(len(engines(t[6])) for c in steps for _, call in steps[c] for t in call if t[7] == sem and core in t[0])

    lo = SQ if r == 0 else 0
    xc = 2 * SQ if r == N - 1 else 3 * SQ
    hi = xc + TC
    c0 = CW * r
    counts = any(what == "cnt" for what, _ in steps[core])

    if counts:
        g.sync.dma_start(T.flc[:], T.fl[:]).then_inc(S.lf, 16)
    g.scalar.dma_start(T.flp[0:16, :], T.fl[:]).then_inc(S.lg, 16)
    g.sync.dma_start(T.win[:, SQ:2 * SQ], T.st[:]).then_inc(S.ls, 16)
    g.sync.dma_start(T.win[:, xc:hi], T.x[:]).then_inc(S.lx, 16)

    g.iota(T.kv[0:16, :], [[0, 8], [1, 16]], 0, -1, allow_small_or_imprecise_dtypes=True).then_inc(S.gi, 1)
    g.iota(T.kj[0:16, :], [[16, 128]], xc - lo, 1, allow_small_or_imprecise_dtypes=True).then_inc(S.gi, 1)
    need = {"cnt": (S.vc, 1), "st": (S.ls, 16), "cin": (S.cin, total("cin")), "rl": (S.rl, total("rl"))}
    loc = 0
    for what, call in steps[core]:
        g.wait_ge(*need[what])
        trs = []
        for ds, sb, sc, db, dc, w, m, sem in call:
            at = [topo.addr(d, core) for d in ds]
            trs.append(RemoteDMATransfer(dst_ids=[DstId(rid=rid, pnc=pid) for rid, pid in at], dma_engine_mask=m,
                                         remote_sem=S[sem], srcs=[T[sb][:, sc:sc + w]],
                                         dsts=[T[db][:, dc:dc + w] for d in ds]))
            loc += len(engines(m))
        g.remote_dma_fused(trs, local_sem=S.loc)

    v, t = g.vector, g.tensor
    v.memset(T.one[:], 1.0).then_inc(S.vk, 1)
    v.memset(T.zero[:], 0.0).then_inc(S.vk, 1)
    v.memset(T.flb[0:16, 0:1], 0.0).then_inc(S.vk, 1)
    v.wait_ge(S.gi, 2)
    v.tensor_scalar(T.kl[0:16, :], T.kv[0:16, :], 0.0, None, A.is_gt).then_inc(S.vk, 1)
    v.tensor_scalar(T.ku[0:16, :], T.kv[0:16, :], 0.0, None, A.is_le).then_inc(S.vk, 1)
    v.tensor_scalar(T.kr[0:16, :], T.kv[0:16, :], 0.0, None, A.is_equal).then_inc(S.vk, 1)
    if counts:
        v.wait_ge(S.lf, 16)
        v.tensor_tensor(T.cnt[:, c0:c0 + CW], T.flc[:, 0:8], T.flc[:, 8:16], A.add).then_inc(S.vc, 1)
    v.wait_ge(S.lg, 16)
    v.tensor_copy(T.flb[0:16, 1:129], T.flp[0:16, :]).then_inc(S.vf, 1)
    v.tensor_scalar(T.nf[0:16, :], T.flp[0:16, :], -1.0, 1.0, A.mult, A.add).then_inc(S.vn, 1)
    v.wait_ge(S.vn, 1)
    v.tensor_tensor(T.uf[0:16, :], T.nf[0:16, :], T.kj[0:16, :], A.mult).then_inc(S.vu, 1)

    t.wait_ge(S.vk, 6)
    t.wait_ge(S.vf, 1)
    t.matmul(T.pd[:, c0:c0 + 128], T.kl[0:16, :], T.flb[0:16, 1:129], True, False).then_inc(S.pe, 1)
    t.matmul(T.pd[:, c0:c0 + 128], T.ku[0:16, :], T.flb[0:16, 0:128], False, True).then_inc(S.pe, 1)
    t.wait_ge(S.vu, 1)
    t.matmul(T.pm[:, 0:128], T.kr[0:16, :], T.uf[0:16, :], True, True).then_inc(S.pem, 1)
    for sem in ("cin", "cf"):
        if total(sem):
            t.wait_ge(S[sem], total(sem))
    if r:
        t.matmul(T.pd[:, 0:c0], T.one[:], T.cnt[:, 0:c0], True, True).then_inc(S.pe, 1)

    v.wait_ge(S.vk, 6)
    v.wait_ge(S.pe, 3 if r else 2)
    v.tensor_tensor_scan(T.sc[:, 0:c0 + 128], T.pd[:, 0:c0 + 128], T.zero[:, 0:c0 + 128],
                         float(-SQ * (r - 1) - lo), A.add, A.add).then_inc(S.vs, 1)
    v.wait_ge(S.pem, 1)
    v.wait_ge(S.vs, 1)
    v.tensor_tensor(T.mx[:], T.sc[:, c0:c0 + 128], T.pm[:, 0:128], A.max).then_inc(S.vm, 1)
    v.wait_ge(S.vm, 1)
    v.tensor_copy(T.off[:], T.mx[:]).then_inc(S.vo, 1)

    for q in (v, g.scalar):
        q.wait_ge(S.vo, 1)
        q.wait_ge(S.ls, 16)
        q.wait_ge(S.lx, 16)
        q.wait_ge(S.nb, total("nb"))
    at, made = 0, []
    for name in ("gv", "ga"):
        for i, w in enumerate(PIECES):
            src = T.win[:, lo:hi].indirect(T.off[:, at // 16:(at + w) // 16])
            sem = S[name + str(i)]
            if name == "gv":
                v.tensor_copy(T.yb[:, at:at + w], src).then_inc(sem, 1)
            else:
                g.scalar.activation(T.yb[:, at:at + w], src, F.Copy).then_inc(sem, 1)
            made.append((i, at, w, sem))
            at += w
    made.sort(key=lambda e: e[:2])
    for i, at, w, sem in made:
        q = g.scalar if (i, at, w, sem) == made[-1] else g.sync
        q.wait_ge(sem, 1)
        q.dma_start(T.y[:, at:at + w], T.yb[:, at:at + w]).then_inc(S.ys, 16)
    g.sync.wait_ge(S.ys, 16 * len(made))
    g.wait_ge(S.loc, loc)
